import numpy as np
import ml_dtypes


def mxq(x, axis, fmt="e4m3"):
    dtype, down = {"e4m3": (ml_dtypes.float8_e4m3fn, 7), "e5m2": (ml_dtypes.float8_e5m2, 14)}[fmt]
    v = np.moveaxis(np.asarray(x, np.float32).astype(ml_dtypes.bfloat16).astype(np.float64), axis, -1)
    blocks = v.reshape(v.shape[:-1] + (-1, 32))
    amax = np.abs(blocks).max(-1, keepdims=True)
    byte = np.maximum(np.where(amax > 0, np.frexp(amax)[1] - 1 + 127, 0) - down, 1)
    scale = np.exp2(byte - 127.0)
    codes = (blocks / scale).astype(np.float32).astype(dtype).astype(np.float64)
    return np.moveaxis((codes * scale).reshape(v.shape), -1, axis)


WIDE = False


def mx_kscale(k):
    if not WIDE:
        return np.ones(k)
    levels = np.array([10, -10, 5, -5, 0])
    if k % 512:
        return np.exp2(np.random.permutation(np.resize(levels, k // 32))).repeat(32)
    a = np.empty((k // 512, 16))
    for p in range(k // 512):
        a[p, :8] = np.random.permutation(np.resize(levels, 8))
        for g in range(8):
            far = levels[np.abs(levels - a[p, g]) >= 10]
            a[p, g + 8] = far[np.random.randint(len(far))]
    return np.exp2(a.ravel()).repeat(32)


def f64(x):
    return np.asarray(x).astype(np.float64)


def striped(idx):
    return np.tile(idx.reshape(-1, 16).T, (8, 1)).astype(np.uint16)


def unstriped(offs):
    return offs[:16].T.reshape(-1).astype(np.int64)


def pack_weight(w):
    k, n = w.shape
    w = f64(np.asarray(w, np.float32).astype(ml_dtypes.bfloat16)).reshape(k // 32, 32, n)
    amax = np.abs(w).max(1)
    byte = np.clip(np.where(amax > 0, np.frexp(amax)[1] - 1 + 127 - 7, 1), 1, 254)
    scaled = (w * np.exp2(127.0 - byte)[:, None, :]).reshape(k, n).astype(np.float32)
    words = np.ascontiguousarray(scaled.reshape(k // 512, 128, 4, n).transpose(0, 1, 3, 2)).astype(ml_dtypes.float8_e4m3fn).view(np.uint8)
    return words, np.ascontiguousarray(byte.astype(np.uint8).reshape(k // 512, 16, n))


def unpack_weight(words, scales):
    g, p, n, _ = words.shape
    vals = np.ascontiguousarray(words).view(ml_dtypes.float8_e4m3fn).astype(np.float64) * np.repeat(np.exp2(scales.astype(np.float64) - 127.0), 8, axis=1)[..., None]
    return vals.transpose(0, 1, 3, 2).reshape(g * 512, n)


def sigmoid(v):
    return 1.0 / (1.0 + np.exp(-np.maximum(v, -700.0)))


K, T, S, D, N, H, V, U = 512, 4096, 1024, 4, 256, 512, 256, 512


def setup_inputs():
    n = np.random.standard_normal
    s = mx_kscale(K)[:, None]
    u = mx_kscale(H)
    packed_xT = pack_weight(n((K, T)) * s)
    return {
        "x_words": packed_xT[0],
        "x_scales": packed_xT[1],
        "w1": (n((K, H)) / np.sqrt(K) / s).astype(np.float32),
        "w2": (n((K, H)) / np.sqrt(K) / s).astype(np.float32),
        "bg": (n((H, U))).astype(np.float32),
        "unit": (np.random.uniform(0.6, 1.4, (H, 1)) * u[:, None]).astype(np.float32),
        "w3": (n((H, N)) / np.sqrt(H) / u[:, None]).astype(np.float32),
        "offs": striped(np.random.permutation(T)[:S]),
        "pix": striped(np.random.permutation(np.concatenate([np.arange(V), np.random.randint(0, V, U - V)]))),
    }


def reference(x_words, x_scales, w1, w2, bg, unit, w3, offs, pix):
    xq = unpack_weight(x_words, x_scales)[:, unstriped(offs)]
    sd = mxq(f64(w1), 0, "e4m3").T @ xq
    cdf = sigmoid(2.5 * sd)
    alf = np.maximum((cdf - (np.pad(cdf, ((0, 0), (0, 1)))[:, 1:])) / (cdf + 0.1), 0.1 * cdf)
    tr = -1.0 * alf + 1.0
    we = alf * (np.pad(tr, ((0, 0), (1, 0)))[:, :S])
    ft = mxq(f64(w2), 0, "e4m3").T @ xq
    wf = we * ft
    ray = wf.reshape(len(wf), -1, D).sum(axis=2)
    cp = ray[:, unstriped(pix)]
    rest = -1.0 * (we.reshape(len(we), -1, D).sum(axis=2)) + 1.0
    hid = f64(unit) * (cp + f64(bg) * rest[:, unstriped(pix)])
    return mxq(f64(w3), 0, "e4m3").T @ mxq(hid, 0, "e4m3")

@@ -1,0 +1,232 @@
+import math
+from contextlib import ExitStack
+
+import concourse.mybir as mybir
+from concourse.masks import make_identity
+
+K, T, S, D, N, H, V, U = 512, 4096, 1024, 4, 256, 512, 256, 512
+FLOPS = 2 * (2 * K * H * S + H * N * U)
+
+F32 = mybir.dt.float32
+BF16 = mybir.dt.bfloat16
+I32 = mybir.dt.int32
+U32 = mybir.dt.uint32
+U16 = mybir.dt.uint16
+U8 = mybir.dt.uint8
+FP8X4 = mybir.dt.float8_e4m3fn_x4
+ACT = mybir.ActivationFunctionType
+ALU = mybir.AluOpType
+
+P = 128
+PACK = 4
+HALF = S // 2
+VH = V // 2
+ROW = V + 8
+WINDOW = U + 16
+UH = U // 2
+
+
+def tile_picked_yneusa_bg_p_kernel(tc, x_words, x_scales, w1, w2, bg, unit, w3, offs, pix, out):
+    nc = tc.nc
+    with ExitStack() as ctx:
+        keep = ctx.enter_context(tc.tile_pool(name="keep", bufs=1))
+        ring = ctx.enter_context(tc.tile_pool(name="ring", bufs=2))
+        psum = ctx.enter_context(tc.psum_pool(name="psum", bufs=1))
+
+        offs_sb = keep.tile([P, S // 16], U16, name="offs_sb")
+        pix_sb = keep.tile([P, U // 16], U16, name="pix_sb")
+        x_table = keep.tile([P, T], I32, name="x_table", align_bytes=64)
+        s_table = keep.tile([P, T], U8, name="s_table", align_bytes=64)
+        w1_raw = keep.tile([P, PACK, H], F32, name="w1_raw")
+        w2_raw = keep.tile([P, PACK, H], F32, name="w2_raw")
+        w3_raw = keep.tile([P, PACK, N], F32, name="w3_raw")
+        bg_sb = keep.tile([P, PACK, U], F32, name="bg_sb")
+        unit_sb = keep.tile([P, PACK], F32, name="unit_sb")
+
+        nc.vector.memset(s_table[:].bitcast(I32), 0)
+        nc.sync.dma_start(offs_sb[:], offs)
+        nc.sync.dma_start(w1_raw[:], w1.rearrange("(p j) c -> p j c", j=PACK))
+        for q in range(4):
+            nc.sync.dma_start(s_table[32 * q : 32 * q + 4, :].bitcast(I32), x_scales[0, 4 * q : 4 * q + 4, :].bitcast(I32))
+        nc.sync.dma_start(x_table[:], x_words[0].rearrange("p c r -> p (c r)").bitcast(I32))
+        nc.sync.dma_start(w2_raw[:], w2.rearrange("(p j) c -> p j c", j=PACK))
+        nc.sync.dma_start(unit_sb[:], unit.rearrange("(p t) o -> p (t o)", t=PACK))
+        nc.sync.dma_start(pix_sb[:], pix)
+        nc.sync.dma_start(bg_sb[:], bg.rearrange("(p t) r -> p t r", t=PACK))
+        nc.sync.dma_start(w3_raw[:], w3.rearrange("(p j) c -> p j c", j=PACK))
+
+        identity = keep.tile([P, P], F32, name="identity")
+        make_identity(nc, identity[:])
+        cdf = [keep.tile([P, D, ROW], F32, name=f"cdf{t}") for t in range(PACK)]
+        alf = [keep.tile([P, D, ROW], F32, name=f"alf{t}") for t in range(PACK)]
+        ray = [keep.tile([P, WINDOW], F32, name=f"ray{t}") for t in range(PACK)]
+        rest = [keep.tile([P, WINDOW], F32, name=f"rest{t}") for t in range(PACK)]
+        for t in range(PACK):
+            nc.gpsimd.memset(cdf[t][:, 0, V : V + 1], 0.0)
+            nc.gpsimd.memset(alf[t][:, D - 1, 7:8], 10.0)
+            nc.gpsimd.memset(ray[t][:, V:], 0.0)
+            nc.gpsimd.memset(rest[t][:, V:], 0.0)
+
+        def deal_weight(name, raw, t0, t1):
+            count = t1 - t0
+            grouped = keep.tile([P, count, P, PACK], BF16, name=name + "_bf", align_bytes=64)
+            nc.scalar.copy(
+                grouped[:].rearrange("p t m j -> p m j t"),
+                raw[:].rearrange("p j (m t) -> p m j t", t=PACK)[:, :, :, t0:t1],
+            )
+            codes = keep.tile([P, count * P], U32, name=name + "_codes", align_bytes=64)
+            scales = keep.tile([P, count * P], U8, name=name + "_scales", align_bytes=64)
+            nc.vector.quantize_mx(out=codes[:].bitcast(FP8X4), scales=scales[:], in_=grouped[:].rearrange("p t m j -> p (t m j)"))
+            return [(codes[:, i * P : (i + 1) * P], scales[:, i * P : (i + 1) * P]) for i in range(count)]
+
+        w1_q = deal_weight("w1", w1_raw, 0, PACK)
+
+        picked = {}
+        for h in (1, 0):
+            words = keep.tile([P, HALF], U32, name=f"words{h}", align_bytes=64)
+            scale_bytes = keep.tile([P, HALF], U8, name=f"bytes{h}", align_bytes=64)
+            entries = offs_sb[:, h * HALF // 16 : (h + 1) * HALF // 16]
+            nc.vector.tensor_copy(words[:], x_table[:].bitcast(U32).indirect(entries))
+            nc.vector.tensor_copy(scale_bytes[:], s_table[:].indirect(entries))
+            picked[h] = (words, scale_bytes)
+
+        def product(weight, h, tag, bufs):
+            bank = psum.tile([P, HALF], F32, name=tag, tag=tag, bufs=bufs)
+            words, scale_bytes = picked[h]
+            nc.tensor.matmul_mx(out=bank[:], lhsT=weight[0].bitcast(FP8X4), lhsT_scale=weight[1],
+                                rhs=words[:].bitcast(FP8X4), rhs_scale=scale_bytes[:], start=True, stop=True)
+            return bank[:].rearrange("p (v d) -> p d v", d=D)
+
+        tail = {}
+
+        def sigmoids(t):
+            tail[t] = ring.tile([P, D, V], F32, name="tail")
+            for h in (1, 0):
+                sd = product(w1_q[t], h, "sd", 3)
+                vs = slice(h * VH, (h + 1) * VH)
+                nc.scalar.activation(cdf[t][:, :, vs], sd, ACT.Sigmoid, scale=2.5)
+                nc.scalar.activation(tail[t][:, :, vs], sd, ACT.Sigmoid, scale=-2.5, bias=-math.log(11.0))
+
+        inv, fall, nwe, wf = {}, {}, {}, {}
+
+        def inverse(t, v0, v1):
+            if t not in inv:
+                inv[t] = ring.tile([P, D, V], F32, name="inv")
+                fall[t] = ring.tile([P, D, V], F32, name="fall")
+            nc.vector.tensor_scalar(inv[t][:, :, v0:v1], tail[t][:, :, v0:v1], 0.1, -1000.0 / 11.0, ALU.add, ALU.mult)
+
+        def ratio(t, v0, v1):
+            nc.vector.scalar_tensor_tensor(fall[t][:, : D - 1, v0:v1], cdf[t][:, 1:, v0:v1], 0.1, inv[t][:, : D - 1, v0:v1], ALU.add, ALU.mult)
+            nc.vector.scalar_tensor_tensor(fall[t][:, D - 1, v0:v1], cdf[t][:, 0, v0 + 1 : v1 + 1], 0.1, inv[t][:, D - 1, v0:v1], ALU.add, ALU.mult)
+
+        def opacity(t, v0, v1):
+            nc.vector.scalar_tensor_tensor(alf[t][:, :, 8 + v0 : 8 + v1], fall[t][:, :, v0:v1], 10.0, cdf[t][:, :, v0:v1], ALU.add, ALU.max)
+
+        def weights(t):
+            nwe[t] = ring.tile([P, D, V], F32, name="nwe")
+            nc.vector.scalar_tensor_tensor(nwe[t][:, 1:, :], alf[t][:, : D - 1, 8:], 10.0, alf[t][:, 1:, 8:], ALU.subtract, ALU.mult)
+            nc.vector.scalar_tensor_tensor(nwe[t][:, 0, :], alf[t][:, D - 1, 7 : 7 + V], 10.0, alf[t][:, 0, 8:], ALU.subtract, ALU.mult)
+
+        def weighted(t, h):
+            if t not in wf:
+                wf[t] = ring.tile([P, D, V], F32, name="wf")
+            ft = product(w2_q[t], h, "ft", 2)
+            vs = slice(h * VH, (h + 1) * VH)
+            nc.vector.scalar_tensor_tensor(wf[t][:, :, vs], nwe[t][:, :, vs], ray_scale[:, t : t + 1], ft, ALU.mult, ALU.mult)
+
+        def ray_sum(source, window, scale, bias):
+            turned = psum.tile([P, 2, P], F32, name="turned", tag="turned", bufs=2)
+            for h in range(2):
+                for d in range(D):
+                    nc.tensor.matmul(turned[:, h, :], source[:, d, h * VH : (h + 1) * VH], identity[:],
+                                     start=(d == 0), stop=(d == D - 1), is_transpose=True)
+            staged = ring.tile([P, 2, P], F32, name="staged")
+            nc.scalar.copy(staged[:], turned[:])
+            back = psum.tile([P, 2, P], F32, name="back", tag="back", bufs=1)
+            for h in range(2):
+                nc.tensor.transpose(back[:, h, :], staged[:, h, :], identity[:])
+            nc.scalar.activation(window[:, :V], back[:].rearrange("p h v -> p (h v)"), ACT.Copy, scale=scale, bias=bias)
+
+        fetched = {}
+
+        def fetch(window, key, r0, r1):
+            if key not in fetched:
+                fetched[key] = ring.tile([P, U], F32, name="fetched_" + key[0])
+            nc.scalar.activation(fetched[key][:, r0:r1], window[:].indirect(pix_sb[:, r0 // 16 : r1 // 16]), ACT.Copy)
+
+        hid = keep.tile([P, PACK, U], F32, name="hid")
+        shade = {}
+
+        def background(t):
+            shade[t] = ring.tile([P, U], F32, name="shade")
+            nc.vector.scalar_tensor_tensor(shade[t][:], fetched["rest", t][:], unit_sb[:, t : t + 1], bg_sb[:, t, :], ALU.mult, ALU.mult)
+
+        def blend(t, r0, r1):
+            nc.vector.tensor_tensor(hid[:, t, r0:r1], fetched["ray", t][:, r0:r1], shade[t][:, r0:r1], ALU.add)
+
+        sigmoids(0)
+        w2_q = deal_weight("w2a", w2_raw, 0, 2)
+        ray_scale = keep.tile([P, PACK], F32, name="ray_scale")
+        nc.vector.tensor_scalar(ray_scale[:], unit_sb[:], -0.01, None, ALU.mult)
+        for h in (1, 0):
+            inverse(0, h * VH, (h + 1) * VH)
+            ratio(0, h * VH, (h + 1) * VH)
+            opacity(0, h * VH, (h + 1) * VH)
+        sigmoids(1)
+        last = PACK - 1
+        for t in range(PACK):
+            ahead = t < last
+            if ahead:
+                inverse(t + 1, 0, V)
+            weights(t)
+            if ahead:
+                ratio(t + 1, 0, V)
+            if t + 2 <= last:
+                sigmoids(t + 2)
+            if t == 0:
+                w2_q = w2_q + deal_weight("w2b", w2_raw, 2, PACK)
+            weighted(t, 0)
+            if ahead:
+                opacity(t + 1, 0, V)
+            weighted(t, 1)
+            ray_sum(nwe[t], rest[t], 0.01, 1.0)
+            fetch(rest[t], ("rest", t), 0, U)
+            if t >= 1:
+                background(t - 1)
+                blend(t - 1, 0, U)
+            if t == 1:
+                w3_bf = keep.tile([P, N, PACK], BF16, name="w3_bf", align_bytes=64)
+                nc.scalar.copy(w3_bf[:].rearrange("p (c i) j -> p c j i", i=4), w3_raw[:].rearrange("p j (c i) -> p c j i", i=4))
+                w3_codes = keep.tile([P, N], U32, name="w3_codes", align_bytes=64)
+                w3_scales = keep.tile([P, N], U8, name="w3_scales", align_bytes=64)
+                nc.vector.quantize_mx(out=w3_codes[:].bitcast(FP8X4), scales=w3_scales[:], in_=w3_bf[:].rearrange("p n j -> p (n j)"))
+            if ahead:
+                ray_sum(wf[t], ray[t], 1.0, 0.0)
+                fetch(ray[t], ("ray", t), 0, U)
+
+        pairs = keep.tile([P, 2, V], F32, name="pairs")
+        nc.vector.tensor_tensor(pairs[:], wf[last][:, :2, :], wf[last][:, 2:, :], ALU.add)
+        background(last)
+        nc.vector.tensor_tensor(ray[last][:, :V], pairs[:, 0, :], pairs[:, 1, :], ALU.add)
+        for h in range(2):
+            fetch(ray[last], ("ray", last), h * UH, (h + 1) * UH)
+        for h in range(2):
+            blend(last, h * UH, (h + 1) * UH)
+        hid_bf = []
+        for h in range(2):
+            rounded = keep.tile([P, UH, PACK], BF16, name=f"hid_bf{h}", align_bytes=64)
+            nc.vector.tensor_copy(rounded[:].rearrange("p (c i) t -> p c t i", i=4),
+                                  hid[:, :, h * UH : (h + 1) * UH].rearrange("p t (c i) -> p c t i", i=4))
+            hid_bf.append(rounded)
+        for h in range(2):
+            codes = keep.tile([P, UH], U32, name=f"hid_codes{h}", align_bytes=64)
+            scales = keep.tile([P, UH], U8, name=f"hid_scales{h}", align_bytes=64)
+            nc.vector.quantize_mx(out=codes[:].bitcast(FP8X4), scales=scales[:], in_=hid_bf[h][:].rearrange("p r t -> p (r t)"))
+            bank = psum.tile([P, N // P, UH], F32, name="colour", tag="sd", bufs=3)
+            for m in range(N // P):
+                nc.tensor.matmul_mx(out=bank[:, m, :], lhsT=w3_codes[:, m * P : (m + 1) * P].bitcast(FP8X4),
+                                    lhsT_scale=w3_scales[:, m * P : (m + 1) * P],
+                                    rhs=codes[:].bitcast(FP8X4), rhs_scale=scales[:], start=True, stop=True)
+            result = keep.tile([P, N // P, UH], F32, name=f"result{h}")
+            nc.scalar.copy(result[:], bank[:])
+            nc.sync.dma_start(out.rearrange("(m p) r -> p m r", p=P)[:, :, h * UH : (h + 1) * UH], result[:])

@@ -58,19 +58,21 @@ def tile_picked_yneusa_bg_p_kernel(tc, x_words, x_scales, w1, w2, bg, unit, w3, 
         identity = keep.tile([P, P], F32, name="identity")
         make_identity(nc, identity[:])
         cdf = [keep.tile([P, D, ROW], F32, name=f"cdf{t}") for t in range(PACK)]
-        alf = [keep.tile([P, D, ROW], F32, name=f"alf{t}") for t in range(PACK)]
+        alf_rows = [keep.tile([P, D + 1, ROW], F32, name=f"alf{t}") for t in range(PACK)]
+        alf = [rows[:, 1:, :] for rows in alf_rows]
         ray = [keep.tile([P, WINDOW], F32, name=f"ray{t}") for t in range(PACK)]
         rest = [keep.tile([P, WINDOW], F32, name=f"rest{t}") for t in range(PACK)]
         for t in range(PACK):
             nc.gpsimd.memset(cdf[t][:, 0, V : V + 1], 0.0)
             nc.gpsimd.memset(alf[t][:, D - 1, 7:8], 10.0)
-            nc.gpsimd.memset(ray[t][:, V:], 0.0)
-            nc.gpsimd.memset(rest[t][:, V:], 0.0)
+            nc.gpsimd.memset(ray[t][:, (2 * V if t < PACK - 2 else V) :], 0.0)
+            nc.gpsimd.memset(rest[t][:, (2 * V if t < PACK - 1 else V) :], 0.0)
+        spare = keep.tile([P, V], F32, name="spare")
 
-        def deal_weight(name, raw, t0, t1):
+        def deal_weight(name, raw, t0, t1, round_copy):
             count = t1 - t0
             grouped = keep.tile([P, count, P, PACK], BF16, name=name + "_bf", align_bytes=64)
-            nc.scalar.copy(
+            round_copy(
                 grouped[:].rearrange("p t m j -> p m j t"),
                 raw[:].rearrange("p j (m t) -> p m j t", t=PACK)[:, :, :, t0:t1],
             )
@@ -79,7 +81,7 @@ def tile_picked_yneusa_bg_p_kernel(tc, x_words, x_scales, w1, w2, bg, unit, w3, 
             nc.vector.quantize_mx(out=codes[:].bitcast(FP8X4), scales=scales[:], in_=grouped[:].rearrange("p t m j -> p (t m j)"))
             return [(codes[:, i * P : (i + 1) * P], scales[:, i * P : (i + 1) * P]) for i in range(count)]
 
-        w1_q = deal_weight("w1", w1_raw, 0, PACK)
+        w1_q = deal_weight("w1a", w1_raw, 0, 2, nc.vector.tensor_copy) + deal_weight("w1b", w1_raw, 2, PACK, nc.vector.tensor_copy)
 
         picked = {}
         for h in (1, 0):
@@ -104,129 +106,149 @@ def tile_picked_yneusa_bg_p_kernel(tc, x_words, x_scales, w1, w2, bg, unit, w3, 
             for h in (1, 0):
                 sd = product(w1_q[t], h, "sd", 3)
                 vs = slice(h * VH, (h + 1) * VH)
-                nc.scalar.activation(cdf[t][:, :, vs], sd, ACT.Sigmoid, scale=2.5)
                 nc.scalar.activation(tail[t][:, :, vs], sd, ACT.Sigmoid, scale=-2.5, bias=-math.log(11.0))
+                nc.scalar.activation(cdf[t][:, :, vs], sd, ACT.Sigmoid, scale=2.5)
 
-        inv, fall, nwe, wf = {}, {}, {}, {}
+        fall, nwe, wf = {}, {}, {}
 
-        def inverse(t, v0, v1):
-            if t not in inv:
-                inv[t] = ring.tile([P, D, V], F32, name="inv")
+        def inverse(engine, dst, src):
+            engine.tensor_scalar(dst, src, -1000.0 / 11.0, -100.0 / 11.0, ALU.mult, ALU.add)
+
+        def ratio(t, inv_head, inv_last, v0, v1):
+            if t not in fall:
                 fall[t] = ring.tile([P, D, V], F32, name="fall")
-            nc.vector.tensor_scalar(inv[t][:, :, v0:v1], tail[t][:, :, v0:v1], 0.1, -1000.0 / 11.0, ALU.add, ALU.mult)
+            nc.vector.scalar_tensor_tensor(fall[t][:, : D - 1, v0:v1], cdf[t][:, 1:, v0:v1], 0.1, inv_head[:, :, v0:v1], ALU.add, ALU.mult)
+            nc.vector.scalar_tensor_tensor(fall[t][:, D - 1, v0:v1], cdf[t][:, 0, v0 + 1 : v1 + 1], 0.1, inv_last[:, v0:v1], ALU.add, ALU.mult)
 
-        def ratio(t, v0, v1):
-            nc.vector.scalar_tensor_tensor(fall[t][:, : D - 1, v0:v1], cdf[t][:, 1:, v0:v1], 0.1, inv[t][:, : D - 1, v0:v1], ALU.add, ALU.mult)
-            nc.vector.scalar_tensor_tensor(fall[t][:, D - 1, v0:v1], cdf[t][:, 0, v0 + 1 : v1 + 1], 0.1, inv[t][:, D - 1, v0:v1], ALU.add, ALU.mult)
-
-        def opacity(t, v0, v1):
-            nc.vector.scalar_tensor_tensor(alf[t][:, :, 8 + v0 : 8 + v1], fall[t][:, :, v0:v1], 10.0, cdf[t][:, :, v0:v1], ALU.add, ALU.max)
+        def opacity(t, v0, v1, rows):
+            for ds in rows:
+                nc.vector.scalar_tensor_tensor(alf[t][:, ds, 8 + v0 : 8 + v1], fall[t][:, ds, v0:v1], 10.0, cdf[t][:, ds, v0:v1], ALU.add, ALU.max)
 
         def weights(t):
             nwe[t] = ring.tile([P, D, V], F32, name="nwe")
-            nc.vector.scalar_tensor_tensor(nwe[t][:, 1:, :], alf[t][:, : D - 1, 8:], 10.0, alf[t][:, 1:, 8:], ALU.subtract, ALU.mult)
+            nc.vector.scalar_tensor_tensor(nwe[t][:, 1:3, :], alf[t][:, 0:2, 8:], 10.0, alf[t][:, 1:3, 8:], ALU.subtract, ALU.mult)
             nc.vector.scalar_tensor_tensor(nwe[t][:, 0, :], alf[t][:, D - 1, 7 : 7 + V], 10.0, alf[t][:, 0, 8:], ALU.subtract, ALU.mult)
+            nc.vector.scalar_tensor_tensor(nwe[t][:, 3, :], alf[t][:, 2, 8:], 10.0, alf[t][:, 3, 8:], ALU.subtract, ALU.mult)
 
-        def weighted(t, h):
+        def weighted(t):
+            wf[t] = ring.tile([P, D, V], F32, name="wf")
+            ft = [product(w2_q[t], h, "ft", 2) for h in range(2)]
+            for ds in (slice(0, D - 1), slice(D - 1, D)):
+                for h in range(2):
+                    vs = slice(h * VH, (h + 1) * VH)
+                    nc.vector.tensor_tensor(wf[t][:, ds, vs], nwe[t][:, ds, vs], ft[h][:, ds, :], ALU.mult)
+
+        def weighted_last(t, h):
             if t not in wf:
                 wf[t] = ring.tile([P, D, V], F32, name="wf")
             ft = product(w2_q[t], h, "ft", 2)
             vs = slice(h * VH, (h + 1) * VH)
-            nc.vector.scalar_tensor_tensor(wf[t][:, :, vs], nwe[t][:, :, vs], ray_scale[:, t : t + 1], ft, ALU.mult, ALU.mult)
+            nc.vector.scalar_tensor_tensor(wf[t][:, :, vs], nwe[t][:, :, vs], unit_scale[:, t : t + 1], ft, ALU.mult, ALU.mult)
 
-        def ray_sum(source, window, scale, bias):
+        def ray_sum(source, window, scale, offset, staged):
             turned = psum.tile([P, 2, P], F32, name="turned", tag="turned", bufs=2)
             for h in range(2):
                 for d in range(D):
                     nc.tensor.matmul(turned[:, h, :], source[:, d, h * VH : (h + 1) * VH], identity[:],
                                      start=(d == 0), stop=(d == D - 1), is_transpose=True)
-            staged = ring.tile([P, 2, P], F32, name="staged")
-            nc.scalar.copy(staged[:], turned[:])
+            nc.scalar.copy(staged, turned[:].rearrange("p h i -> p (h i)"))
             back = psum.tile([P, 2, P], F32, name="back", tag="back", bufs=1)
             for h in range(2):
-                nc.tensor.transpose(back[:, h, :], staged[:, h, :], identity[:])
-            nc.scalar.activation(window[:, :V], back[:].rearrange("p h v -> p (h v)"), ACT.Copy, scale=scale, bias=bias)
+                nc.tensor.transpose(back[:, h, :], staged[:, h * P : (h + 1) * P], identity[:])
+            nc.scalar.activation(window[:, :V], back[:].rearrange("p h v -> p (h v)"), ACT.Copy, scale=scale, bias=offset)
 
-        fetched = {}
+        fetched = {"ray": keep.tile([P, PACK, U], F32, name="ray_at"), "rest": keep.tile([P, PACK, U], F32, name="rest_at")}
 
         def fetch(window, key, r0, r1):
-            if key not in fetched:
-                fetched[key] = ring.tile([P, U], F32, name="fetched_" + key[0])
-            nc.scalar.activation(fetched[key][:, r0:r1], window[:].indirect(pix_sb[:, r0 // 16 : r1 // 16]), ACT.Copy)
+            nc.scalar.activation(fetched[key[0]][:, key[1], r0:r1], window[:].indirect(pix_sb[:, r0 // 16 : r1 // 16]), ACT.Copy)
 
-        hid = keep.tile([P, PACK, U], F32, name="hid")
-        shade = {}
+        shade = keep.tile([P, PACK, U], F32, name="shade")
 
         def background(t):
-            shade[t] = ring.tile([P, U], F32, name="shade")
-            nc.vector.scalar_tensor_tensor(shade[t][:], fetched["rest", t][:], unit_sb[:, t : t + 1], bg_sb[:, t, :], ALU.mult, ALU.mult)
+            nc.vector.scalar_tensor_tensor(shade[:, t, :], fetched["rest"][:, t, :], unit_scale[:, t : t + 1], bg_sb[:, t, :], ALU.mult, ALU.mult)
 
-        def blend(t, r0, r1):
-            nc.vector.tensor_tensor(hid[:, t, r0:r1], fetched["ray", t][:, r0:r1], shade[t][:, r0:r1], ALU.add)
+        def pair_sum(source, v0, v1):
+            pairs = ring.tile([P, 2, v1 - v0], F32, name="pairs", bufs=3)
+            nc.vector.tensor_tensor(pairs[:], source[:, :2, v0:v1], source[:, 2:, v0:v1], ALU.add)
+            return pairs
+
+        def pair_total(pairs, window, offset, v0, v1):
+            nc.vector.scalar_tensor_tensor(window[:, v0:v1], pairs[:, 0, :], offset, pairs[:, 1, :], ALU.add, ALU.add)
 
         sigmoids(0)
-        w2_q = deal_weight("w2a", w2_raw, 0, 2)
-        ray_scale = keep.tile([P, PACK], F32, name="ray_scale")
-        nc.vector.tensor_scalar(ray_scale[:], unit_sb[:], -0.01, None, ALU.mult)
-        for h in (1, 0):
-            inverse(0, h * VH, (h + 1) * VH)
-            ratio(0, h * VH, (h + 1) * VH)
-            opacity(0, h * VH, (h + 1) * VH)
+        w2_q = deal_weight("w2a", w2_raw, 0, 2, nc.scalar.copy)
+        unit_scale = keep.tile([P, PACK], F32, name="unit_scale")
+        nc.gpsimd.tensor_scalar(unit_scale[:], unit_sb[:], 0.01, 0.0, ALU.mult, ALU.add)
+        inv_first = keep.tile([P, D, V], F32, name="inv_first")
+        inverse(nc.vector, inv_first[:, :, VH:], tail[0][:, :, VH:])
+        ratio(0, inv_first[:, : D - 1, :], inv_first[:, D - 1, :], VH, V)
+        inverse(nc.vector, inv_first[:, :, :VH], tail[0][:, :, :VH])
+        opacity(0, VH, V, (slice(0, D),))
+        ratio(0, inv_first[:, : D - 1, :], inv_first[:, D - 1, :], 0, VH)
+        opacity(0, 0, VH, (slice(0, D - 1), slice(D - 1, D)))
         sigmoids(1)
         last = PACK - 1
-        for t in range(PACK):
-            ahead = t < last
-            if ahead:
-                inverse(t + 1, 0, V)
+        for t in range(last):
             weights(t)
-            if ahead:
-                ratio(t + 1, 0, V)
+            inv_head = alf_rows[t][:, : D - 1, 8:]
+            inverse(nc.gpsimd, inv_head, tail[t + 1][:, : D - 1, :])
+            weighted(t)
+            inv_last = ring.tile([P, V], F32, name="inv_last")
+            inverse(nc.vector, inv_last[:], tail[t + 1][:, D - 1, :])
+            ray_sum(nwe[t], rest[t], 1.0, 100.0, ray[t - 1][:, V : 2 * V] if t >= 1 else spare[:])
+            if t >= 1:
+                fetch(ray[t - 1], ("ray", t - 1), 0, U)
             if t + 2 <= last:
                 sigmoids(t + 2)
-            if t == 0:
-                w2_q = w2_q + deal_weight("w2b", w2_raw, 2, PACK)
-            weighted(t, 0)
-            if ahead:
-                opacity(t + 1, 0, V)
-            weighted(t, 1)
-            ray_sum(nwe[t], rest[t], 0.01, 1.0)
-            fetch(rest[t], ("rest", t), 0, U)
+            ratio(t + 1, inv_head, inv_last, 0, V)
             if t >= 1:
                 background(t - 1)
-                blend(t - 1, 0, U)
+            opacity(t + 1, 0, V, (slice(0, D - 1), slice(D - 1, D)))
+            ray_sum(wf[t], ray[t], unit_scale[:, t : t + 1], 0.0, rest[t][:, V : 2 * V])
+            fetch(rest[t], ("rest", t), 0, U)
+            if t == 0:
+                w2_q = w2_q + deal_weight("w2b", w2_raw, 2, PACK, nc.scalar.copy)
             if t == 1:
                 w3_bf = keep.tile([P, N, PACK], BF16, name="w3_bf", align_bytes=64)
-                nc.scalar.copy(w3_bf[:].rearrange("p (c i) j -> p c j i", i=4), w3_raw[:].rearrange("p j (c i) -> p c j i", i=4))
+                nc.vector.tensor_copy(w3_bf[:].rearrange("p (c i) j -> p c j i", i=4), w3_raw[:].rearrange("p j (c i) -> p c j i", i=4))
                 w3_codes = keep.tile([P, N], U32, name="w3_codes", align_bytes=64)
                 w3_scales = keep.tile([P, N], U8, name="w3_scales", align_bytes=64)
                 nc.vector.quantize_mx(out=w3_codes[:].bitcast(FP8X4), scales=w3_scales[:], in_=w3_bf[:].rearrange("p n j -> p (n j)"))
-            if ahead:
-                ray_sum(wf[t], ray[t], 1.0, 0.0)
-                fetch(ray[t], ("ray", t), 0, U)
 
-        pairs = keep.tile([P, 2, V], F32, name="pairs")
-        nc.vector.tensor_tensor(pairs[:], wf[last][:, :2, :], wf[last][:, 2:, :], ALU.add)
+        fetch(ray[last - 1], ("ray", last - 1), 0, U)
+        weights(last)
+        background(last - 1)
+        rest_pairs = pair_sum(nwe[last], 0, V)
+        weighted_last(last, 0)
+        pair_total(rest_pairs, rest[last], 100.0, 0, V)
+        fetch(rest[last], ("rest", last), 0, U)
+        weighted_last(last, 1)
+        ray_pairs = [pair_sum(wf[last], h * VH, (h + 1) * VH) for h in range(2)]
+        for h in range(2):
+            pair_total(ray_pairs[h], ray[last], 0.0, h * VH, (h + 1) * VH)
         background(last)
-        nc.vector.tensor_tensor(ray[last][:, :V], pairs[:, 0, :], pairs[:, 1, :], ALU.add)
         for h in range(2):
             fetch(ray[last], ("ray", last), h * UH, (h + 1) * UH)
-        for h in range(2):
-            blend(last, h * UH, (h + 1) * UH)
         hid_bf = []
         for h in range(2):
             rounded = keep.tile([P, UH, PACK], BF16, name=f"hid_bf{h}", align_bytes=64)
-            nc.vector.tensor_copy(rounded[:].rearrange("p (c i) t -> p c t i", i=4),
-                                  hid[:, :, h * UH : (h + 1) * UH].rearrange("p t (c i) -> p c t i", i=4))
+            nc.vector.tensor_tensor(rounded[:].rearrange("p (c i) t -> p c t i", i=4),
+                                    shade[:, :, h * UH : (h + 1) * UH].rearrange("p t (c i) -> p c t i", i=4),
+                                    fetched["ray"][:, :, h * UH : (h + 1) * UH].rearrange("p t (c i) -> p c t i", i=4), ALU.subtract)
             hid_bf.append(rounded)
         for h in range(2):
             codes = keep.tile([P, UH], U32, name=f"hid_codes{h}", align_bytes=64)
             scales = keep.tile([P, UH], U8, name=f"hid_scales{h}", align_bytes=64)
             nc.vector.quantize_mx(out=codes[:].bitcast(FP8X4), scales=scales[:], in_=hid_bf[h][:].rearrange("p r t -> p (r t)"))
-            bank = psum.tile([P, N // P, UH], F32, name="colour", tag="sd", bufs=3)
             for m in range(N // P):
-                nc.tensor.matmul_mx(out=bank[:, m, :], lhsT=w3_codes[:, m * P : (m + 1) * P].bitcast(FP8X4),
+                tag, bufs = (("sd", 3), ("ft", 2))[m]
+                bank = psum.tile([P, UH], F32, name="colour", tag=tag, bufs=bufs)
+                nc.tensor.matmul_mx(out=bank[:], lhsT=w3_codes[:, m * P : (m + 1) * P].bitcast(FP8X4),
                                     lhsT_scale=w3_scales[:, m * P : (m + 1) * P],
                                     rhs=codes[:].bitcast(FP8X4), rhs_scale=scales[:], start=True, stop=True)
-            result = keep.tile([P, N // P, UH], F32, name=f"result{h}")
-            nc.scalar.copy(result[:], bank[:])
-            nc.sync.dma_start(out.rearrange("(m p) r -> p m r", p=P)[:, :, h * UH : (h + 1) * UH], result[:])
+                result = keep.tile([P, UH], F32, name=f"result{h}{m}")
+                if h == 1 and m == 1:
+                    nc.vector.tensor_copy(result[:], bank[:])
+                else:
+                    nc.scalar.copy(result[:], bank[:])
+                nc.sync.dma_start(out[m * P : (m + 1) * P, h * UH : (h + 1) * UH], result[:])

@@ -19,11 +19,15 @@ ALU = mybir.AluOpType
 
 P = 128
 PACK = 4
+LAST = PACK - 1
+PER_COLUMN = 16
 HALF = S // 2
 VH = V // 2
-ROW = V + 8
+PAD = 8
 WINDOW = U + 16
-UH = U // 2
+SD_BANKS, FT_BANKS, TURN_BANKS, BACK_BANKS = 3, 2, 2, 1
+HEAD_ROWS, LAST_ROW = slice(0, D - 1), slice(D - 1, D)
+PIECES = ((0, 128), (128, 384), (384, 512))
 
 
 def tile_picked_yneusa_bg_p_kernel(tc, x_words, x_scales, w1, w2, bg, unit, w3, offs, pix, out):
@@ -33,8 +37,8 @@ def tile_picked_yneusa_bg_p_kernel(tc, x_words, x_scales, w1, w2, bg, unit, w3, 
         ring = ctx.enter_context(tc.tile_pool(name="ring", bufs=2))
         psum = ctx.enter_context(tc.psum_pool(name="psum", bufs=1))
 
-        offs_sb = keep.tile([P, S // 16], U16, name="offs_sb")
-        pix_sb = keep.tile([P, U // 16], U16, name="pix_sb")
+        offs_sb = keep.tile([P, S // PER_COLUMN], U16, name="offs_sb")
+        pix_sb = keep.tile([P, U // PER_COLUMN], U16, name="pix_sb")
         x_table = keep.tile([P, T], I32, name="x_table", align_bytes=64)
         s_table = keep.tile([P, T], U8, name="s_table", align_bytes=64)
         w1_raw = keep.tile([P, PACK, H], F32, name="w1_raw")
@@ -57,198 +61,202 @@ def tile_picked_yneusa_bg_p_kernel(tc, x_words, x_scales, w1, w2, bg, unit, w3, 
 
         identity = keep.tile([P, P], F32, name="identity")
         make_identity(nc, identity[:])
-        cdf = [keep.tile([P, D, ROW], F32, name=f"cdf{t}") for t in range(PACK)]
-        alf_rows = [keep.tile([P, D + 1, ROW], F32, name=f"alf{t}") for t in range(PACK)]
+        cdf = [keep.tile([P, D, V + PAD], F32, name=f"cdf{t}") for t in range(PACK)]
+        alf_rows = [keep.tile([P, D + 1, PAD + V], F32, name=f"alf{t}") for t in range(PACK)]
         alf = [rows[:, 1:, :] for rows in alf_rows]
         ray = [keep.tile([P, WINDOW], F32, name=f"ray{t}") for t in range(PACK)]
         rest = [keep.tile([P, WINDOW], F32, name=f"rest{t}") for t in range(PACK)]
         for t in range(PACK):
             nc.gpsimd.memset(cdf[t][:, 0, V : V + 1], 0.0)
-            nc.gpsimd.memset(alf[t][:, D - 1, 7:8], 10.0)
-            nc.gpsimd.memset(ray[t][:, (2 * V if t < PACK - 2 else V) :], 0.0)
-            nc.gpsimd.memset(rest[t][:, (2 * V if t < PACK - 1 else V) :], 0.0)
-        spare = keep.tile([P, V], F32, name="spare")
+            nc.gpsimd.memset(alf[t][:, D - 1, PAD - 1 : PAD], 10.0)
+            nc.gpsimd.memset(ray[t][:, (2 * V if t + 1 < LAST else V) :], 0.0)
+            nc.gpsimd.memset(rest[t][:, (2 * V if t < LAST else V) :], 0.0)
+        first_staged = keep.tile([P, V], F32, name="first_staged")
 
-        def deal_weight(name, raw, t0, t1, round_copy):
-            count = t1 - t0
-            grouped = keep.tile([P, count, P, PACK], BF16, name=name + "_bf", align_bytes=64)
+        def quantise(name, grouped):
+            columns = grouped.shape[1] // PACK
+            codes = keep.tile([P, columns], U32, name=name + "_codes", align_bytes=64)
+            scales = keep.tile([P, columns], U8, name=name + "_scales", align_bytes=64)
+            nc.vector.quantize_mx(out=codes[:].bitcast(FP8X4), scales=scales[:], in_=grouped)
+            return codes, scales
+
+        def deal_plane_pair(name, raw, t0, round_copy):
+            grouped = keep.tile([P, 2, P, PACK], BF16, name=name + "_bf", align_bytes=64)
             round_copy(
                 grouped[:].rearrange("p t m j -> p m j t"),
-                raw[:].rearrange("p j (m t) -> p m j t", t=PACK)[:, :, :, t0:t1],
+                raw[:].rearrange("p j (m t) -> p m j t", t=PACK)[:, :, :, t0 : t0 + 2],
             )
-            codes = keep.tile([P, count * P], U32, name=name + "_codes", align_bytes=64)
-            scales = keep.tile([P, count * P], U8, name=name + "_scales", align_bytes=64)
-            nc.vector.quantize_mx(out=codes[:].bitcast(FP8X4), scales=scales[:], in_=grouped[:].rearrange("p t m j -> p (t m j)"))
-            return [(codes[:, i * P : (i + 1) * P], scales[:, i * P : (i + 1) * P]) for i in range(count)]
+            codes, scales = quantise(name, grouped[:].rearrange("p t m j -> p (t m j)"))
+            return [(codes[:, i * P : (i + 1) * P], scales[:, i * P : (i + 1) * P]) for i in range(2)]
 
-        w1_q = deal_weight("w1a", w1_raw, 0, 2, nc.vector.tensor_copy) + deal_weight("w1b", w1_raw, 2, PACK, nc.vector.tensor_copy)
+        w1_q = deal_plane_pair("w1a", w1_raw, 0, nc.vector.tensor_copy) + deal_plane_pair("w1b", w1_raw, 2, nc.vector.tensor_copy)
 
         picked = {}
         for h in (1, 0):
             words = keep.tile([P, HALF], U32, name=f"words{h}", align_bytes=64)
             scale_bytes = keep.tile([P, HALF], U8, name=f"bytes{h}", align_bytes=64)
-            entries = offs_sb[:, h * HALF // 16 : (h + 1) * HALF // 16]
+            entries = offs_sb[:, h * HALF // PER_COLUMN : (h + 1) * HALF // PER_COLUMN]
             nc.vector.tensor_copy(words[:], x_table[:].bitcast(U32).indirect(entries))
             nc.vector.tensor_copy(scale_bytes[:], s_table[:].indirect(entries))
             picked[h] = (words, scale_bytes)
 
-        def product(weight, h, tag, bufs):
-            bank = psum.tile([P, HALF], F32, name=tag, tag=tag, bufs=bufs)
+        def product(weight, h, tag, banks):
+            bank = psum.tile([P, HALF], F32, name=tag, tag=tag, bufs=banks)
             words, scale_bytes = picked[h]
             nc.tensor.matmul_mx(out=bank[:], lhsT=weight[0].bitcast(FP8X4), lhsT_scale=weight[1],
                                 rhs=words[:].bitcast(FP8X4), rhs_scale=scale_bytes[:], start=True, stop=True)
             return bank[:].rearrange("p (v d) -> p d v", d=D)
 
-        tail = {}
+        tail, fall, nwe, wf = {}, {}, {}, {}
 
         def sigmoids(t):
             tail[t] = ring.tile([P, D, V], F32, name="tail")
             for h in (1, 0):
-                sd = product(w1_q[t], h, "sd", 3)
-                vs = slice(h * VH, (h + 1) * VH)
-                nc.scalar.activation(tail[t][:, :, vs], sd, ACT.Sigmoid, scale=-2.5, bias=-math.log(11.0))
-                nc.scalar.activation(cdf[t][:, :, vs], sd, ACT.Sigmoid, scale=2.5)
+                sd = product(w1_q[t], h, "sd", SD_BANKS)
+                rays = slice(h * VH, (h + 1) * VH)
+                nc.scalar.activation(tail[t][:, :, rays], sd, ACT.Sigmoid, scale=-2.5, bias=-math.log(11.0))
+                nc.scalar.activation(cdf[t][:, :, rays], sd, ACT.Sigmoid, scale=2.5)
 
-        fall, nwe, wf = {}, {}, {}
-
-        def inverse(engine, dst, src):
-            engine.tensor_scalar(dst, src, -1000.0 / 11.0, -100.0 / 11.0, ALU.mult, ALU.add)
+        def inverse(engine, inv, tail_part):
+            engine.tensor_scalar(inv, tail_part, -1000.0 / 11.0, -100.0 / 11.0, ALU.mult, ALU.add)
 
         def ratio(t, inv_head, inv_last, v0, v1):
             if t not in fall:
                 fall[t] = ring.tile([P, D, V], F32, name="fall")
-            nc.vector.scalar_tensor_tensor(fall[t][:, : D - 1, v0:v1], cdf[t][:, 1:, v0:v1], 0.1, inv_head[:, :, v0:v1], ALU.add, ALU.mult)
+            nc.vector.scalar_tensor_tensor(fall[t][:, HEAD_ROWS, v0:v1], cdf[t][:, 1:, v0:v1], 0.1, inv_head[:, :, v0:v1], ALU.add, ALU.mult)
             nc.vector.scalar_tensor_tensor(fall[t][:, D - 1, v0:v1], cdf[t][:, 0, v0 + 1 : v1 + 1], 0.1, inv_last[:, v0:v1], ALU.add, ALU.mult)
 
-        def opacity(t, v0, v1, rows):
-            for ds in rows:
-                nc.vector.scalar_tensor_tensor(alf[t][:, ds, 8 + v0 : 8 + v1], fall[t][:, ds, v0:v1], 10.0, cdf[t][:, ds, v0:v1], ALU.add, ALU.max)
+        def opacity(t, v0, v1, row_runs):
+            for rows in row_runs:
+                nc.vector.scalar_tensor_tensor(alf[t][:, rows, PAD + v0 : PAD + v1], fall[t][:, rows, v0:v1], 10.0, cdf[t][:, rows, v0:v1], ALU.add, ALU.max)
 
         def weights(t):
             nwe[t] = ring.tile([P, D, V], F32, name="nwe")
-            nc.vector.scalar_tensor_tensor(nwe[t][:, 1:3, :], alf[t][:, 0:2, 8:], 10.0, alf[t][:, 1:3, 8:], ALU.subtract, ALU.mult)
-            nc.vector.scalar_tensor_tensor(nwe[t][:, 0, :], alf[t][:, D - 1, 7 : 7 + V], 10.0, alf[t][:, 0, 8:], ALU.subtract, ALU.mult)
-            nc.vector.scalar_tensor_tensor(nwe[t][:, 3, :], alf[t][:, 2, 8:], 10.0, alf[t][:, 3, 8:], ALU.subtract, ALU.mult)
+            nc.vector.scalar_tensor_tensor(nwe[t][:, 1:3, :], alf[t][:, 0:2, PAD:], 10.0, alf[t][:, 1:3, PAD:], ALU.subtract, ALU.mult)
+            nc.vector.scalar_tensor_tensor(nwe[t][:, 0, :], alf[t][:, D - 1, PAD - 1 : PAD - 1 + V], 10.0, alf[t][:, 0, PAD:], ALU.subtract, ALU.mult)
+            nc.vector.scalar_tensor_tensor(nwe[t][:, 3, :], alf[t][:, 2, PAD:], 10.0, alf[t][:, 3, PAD:], ALU.subtract, ALU.mult)
 
-        def weighted(t):
+        def weighted_features(t):
             wf[t] = ring.tile([P, D, V], F32, name="wf")
-            ft = [product(w2_q[t], h, "ft", 2) for h in range(2)]
-            for ds in (slice(0, D - 1), slice(D - 1, D)):
+            ft = [product(w2_q[t], h, "ft", FT_BANKS) for h in range(2)]
+            for rows in (HEAD_ROWS, LAST_ROW):
                 for h in range(2):
-                    vs = slice(h * VH, (h + 1) * VH)
-                    nc.vector.tensor_tensor(wf[t][:, ds, vs], nwe[t][:, ds, vs], ft[h][:, ds, :], ALU.mult)
+                    rays = slice(h * VH, (h + 1) * VH)
+                    nc.vector.tensor_tensor(wf[t][:, rows, rays], nwe[t][:, rows, rays], ft[h][:, rows, :], ALU.mult)
 
-        def weighted_last(t, h):
-            if t not in wf:
-                wf[t] = ring.tile([P, D, V], F32, name="wf")
-            ft = product(w2_q[t], h, "ft", 2)
-            vs = slice(h * VH, (h + 1) * VH)
-            nc.vector.scalar_tensor_tensor(wf[t][:, :, vs], nwe[t][:, :, vs], unit_scale[:, t : t + 1], ft, ALU.mult, ALU.mult)
-
-        def ray_sum(source, window, scale, offset, staged):
-            turned = psum.tile([P, 2, P], F32, name="turned", tag="turned", bufs=2)
+        def turned_sum(members, window, scale, offset, staged):
+            turned = psum.tile([P, 2, P], F32, name="turned", tag="turned", bufs=TURN_BANKS)
             for h in range(2):
                 for d in range(D):
-                    nc.tensor.matmul(turned[:, h, :], source[:, d, h * VH : (h + 1) * VH], identity[:],
+                    nc.tensor.matmul(turned[:, h, :], members[:, d, h * VH : (h + 1) * VH], identity[:],
                                      start=(d == 0), stop=(d == D - 1), is_transpose=True)
             nc.scalar.copy(staged, turned[:].rearrange("p h i -> p (h i)"))
-            back = psum.tile([P, 2, P], F32, name="back", tag="back", bufs=1)
+            back = psum.tile([P, 2, P], F32, name="back", tag="back", bufs=BACK_BANKS)
             for h in range(2):
                 nc.tensor.transpose(back[:, h, :], staged[:, h * P : (h + 1) * P], identity[:])
             nc.scalar.activation(window[:, :V], back[:].rearrange("p h v -> p (h v)"), ACT.Copy, scale=scale, bias=offset)
 
-        fetched = {"ray": keep.tile([P, PACK, U], F32, name="ray_at"), "rest": keep.tile([P, PACK, U], F32, name="rest_at")}
-
-        def fetch(window, key, r0, r1):
-            nc.scalar.activation(fetched[key[0]][:, key[1], r0:r1], window[:].indirect(pix_sb[:, r0 // 16 : r1 // 16]), ACT.Copy)
-
+        ray_at = keep.tile([P, PACK, U], F32, name="ray_at")
+        rest_at = keep.tile([P, PACK, U], F32, name="rest_at")
         shade = keep.tile([P, PACK, U], F32, name="shade")
 
-        def background(t):
-            nc.vector.scalar_tensor_tensor(shade[:, t, :], fetched["rest"][:, t, :], unit_scale[:, t : t + 1], bg_sb[:, t, :], ALU.mult, ALU.mult)
+        def fetch(target, window, t, r0, r1):
+            nc.scalar.activation(target[:, t, r0:r1], window[:].indirect(pix_sb[:, r0 // PER_COLUMN : r1 // PER_COLUMN]), ACT.Copy)
 
-        def pair_sum(source, v0, v1):
+        def background(t):
+            nc.vector.scalar_tensor_tensor(shade[:, t, :], rest_at[:, t, :], unit_scale[:, t : t + 1], bg_sb[:, t, :], ALU.mult, ALU.mult)
+
+        def pair_sum(members, v0, v1):
             pairs = ring.tile([P, 2, v1 - v0], F32, name="pairs", bufs=3)
-            nc.vector.tensor_tensor(pairs[:], source[:, :2, v0:v1], source[:, 2:, v0:v1], ALU.add)
+            nc.vector.tensor_tensor(pairs[:], members[:, :2, v0:v1], members[:, 2:, v0:v1], ALU.add)
             return pairs
 
         def pair_total(pairs, window, offset, v0, v1):
             nc.vector.scalar_tensor_tensor(window[:, v0:v1], pairs[:, 0, :], offset, pairs[:, 1, :], ALU.add, ALU.add)
 
         sigmoids(0)
-        w2_q = deal_weight("w2a", w2_raw, 0, 2, nc.scalar.copy)
+        w2_q = deal_plane_pair("w2a", w2_raw, 0, nc.scalar.copy)
         unit_scale = keep.tile([P, PACK], F32, name="unit_scale")
         nc.gpsimd.tensor_scalar(unit_scale[:], unit_sb[:], 0.01, 0.0, ALU.mult, ALU.add)
         inv_first = keep.tile([P, D, V], F32, name="inv_first")
         inverse(nc.vector, inv_first[:, :, VH:], tail[0][:, :, VH:])
-        ratio(0, inv_first[:, : D - 1, :], inv_first[:, D - 1, :], VH, V)
+        ratio(0, inv_first[:, HEAD_ROWS, :], inv_first[:, D - 1, :], VH, V)
         inverse(nc.vector, inv_first[:, :, :VH], tail[0][:, :, :VH])
         opacity(0, VH, V, (slice(0, D),))
-        ratio(0, inv_first[:, : D - 1, :], inv_first[:, D - 1, :], 0, VH)
-        opacity(0, 0, VH, (slice(0, D - 1), slice(D - 1, D)))
+        ratio(0, inv_first[:, HEAD_ROWS, :], inv_first[:, D - 1, :], 0, VH)
+        opacity(0, 0, VH, (HEAD_ROWS, LAST_ROW))
         sigmoids(1)
-        last = PACK - 1
-        for t in range(last):
+
+        for t in range(LAST):
             weights(t)
-            inv_head = alf_rows[t][:, : D - 1, 8:]
-            inverse(nc.gpsimd, inv_head, tail[t + 1][:, : D - 1, :])
-            weighted(t)
+            inv_head = alf_rows[t][:, HEAD_ROWS, PAD:]
+            inverse(nc.gpsimd, inv_head, tail[t + 1][:, HEAD_ROWS, :])
+            weighted_features(t)
             inv_last = ring.tile([P, V], F32, name="inv_last")
             inverse(nc.vector, inv_last[:], tail[t + 1][:, D - 1, :])
-            ray_sum(nwe[t], rest[t], 1.0, 100.0, ray[t - 1][:, V : 2 * V] if t >= 1 else spare[:])
+            turned_sum(nwe[t], rest[t], 1.0, 100.0, ray[t - 1][:, V : 2 * V] if t >= 1 else first_staged[:])
             if t >= 1:
-                fetch(ray[t - 1], ("ray", t - 1), 0, U)
-            if t + 2 <= last:
+                fetch(ray_at, ray[t - 1], t - 1, 0, U)
+            if t + 2 <= LAST:
                 sigmoids(t + 2)
             ratio(t + 1, inv_head, inv_last, 0, V)
             if t >= 1:
                 background(t - 1)
-            opacity(t + 1, 0, V, (slice(0, D - 1), slice(D - 1, D)))
-            ray_sum(wf[t], ray[t], unit_scale[:, t : t + 1], 0.0, rest[t][:, V : 2 * V])
-            fetch(rest[t], ("rest", t), 0, U)
+            opacity(t + 1, 0, V, (HEAD_ROWS, LAST_ROW))
+            turned_sum(wf[t], ray[t], unit_scale[:, t : t + 1], 0.0, rest[t][:, V : 2 * V])
+            fetch(rest_at, rest[t], t, 0, U)
             if t == 0:
-                w2_q = w2_q + deal_weight("w2b", w2_raw, 2, PACK, nc.scalar.copy)
-            if t == 1:
-                w3_bf = keep.tile([P, N, PACK], BF16, name="w3_bf", align_bytes=64)
-                nc.vector.tensor_copy(w3_bf[:].rearrange("p (c i) j -> p c j i", i=4), w3_raw[:].rearrange("p j (c i) -> p c j i", i=4))
-                w3_codes = keep.tile([P, N], U32, name="w3_codes", align_bytes=64)
-                w3_scales = keep.tile([P, N], U8, name="w3_scales", align_bytes=64)
-                nc.vector.quantize_mx(out=w3_codes[:].bitcast(FP8X4), scales=w3_scales[:], in_=w3_bf[:].rearrange("p n j -> p (n j)"))
+                w2_q = w2_q + deal_plane_pair("w2b", w2_raw, 2, nc.scalar.copy)
 
-        fetch(ray[last - 1], ("ray", last - 1), 0, U)
-        weights(last)
-        background(last - 1)
-        rest_pairs = pair_sum(nwe[last], 0, V)
-        weighted_last(last, 0)
-        pair_total(rest_pairs, rest[last], 100.0, 0, V)
-        fetch(rest[last], ("rest", last), 0, U)
-        weighted_last(last, 1)
-        ray_pairs = [pair_sum(wf[last], h * VH, (h + 1) * VH) for h in range(2)]
+        w3_bf = keep.tile([P, N, PACK], BF16, name="w3_bf", align_bytes=64)
+        nc.scalar.copy(w3_bf[:].rearrange("p (c i) j -> p c j i", i=4), w3_raw[:].rearrange("p j (c i) -> p c j i", i=4))
+        w3_codes, w3_scales = quantise("w3", w3_bf[:].rearrange("p n j -> p (n j)"))
+
+        fetch(ray_at, ray[LAST - 1], LAST - 1, 0, U)
+        weights(LAST)
+        background(LAST - 1)
+        wf[LAST] = ring.tile([P, D, V], F32, name="wf")
+
+        def weighted_features_last(h):
+            ft = product(w2_q[LAST], h, "ft", FT_BANKS)
+            rays = slice(h * VH, (h + 1) * VH)
+            nc.vector.scalar_tensor_tensor(wf[LAST][:, :, rays], nwe[LAST][:, :, rays], unit_scale[:, LAST : LAST + 1], ft, ALU.mult, ALU.mult)
+
+        rest_pairs = pair_sum(nwe[LAST], 0, V)
+        weighted_features_last(0)
+        pair_total(rest_pairs, rest[LAST], 100.0, 0, V)
+        fetch(rest_at, rest[LAST], LAST, 0, U)
+        weighted_features_last(1)
+        ray_pairs = [pair_sum(wf[LAST], h * VH, (h + 1) * VH) for h in range(2)]
         for h in range(2):
-            pair_total(ray_pairs[h], ray[last], 0.0, h * VH, (h + 1) * VH)
-        background(last)
-        for h in range(2):
-            fetch(ray[last], ("ray", last), h * UH, (h + 1) * UH)
-        hid_bf = []
-        for h in range(2):
-            rounded = keep.tile([P, UH, PACK], BF16, name=f"hid_bf{h}", align_bytes=64)
-            nc.vector.tensor_tensor(rounded[:].rearrange("p (c i) t -> p c t i", i=4),
-                                    shade[:, :, h * UH : (h + 1) * UH].rearrange("p t (c i) -> p c t i", i=4),
-                                    fetched["ray"][:, :, h * UH : (h + 1) * UH].rearrange("p t (c i) -> p c t i", i=4), ALU.subtract)
-            hid_bf.append(rounded)
-        for h in range(2):
-            codes = keep.tile([P, UH], U32, name=f"hid_codes{h}", align_bytes=64)
-            scales = keep.tile([P, UH], U8, name=f"hid_scales{h}", align_bytes=64)
-            nc.vector.quantize_mx(out=codes[:].bitcast(FP8X4), scales=scales[:], in_=hid_bf[h][:].rearrange("p r t -> p (r t)"))
-            for m in range(N // P):
-                tag, bufs = (("sd", 3), ("ft", 2))[m]
-                bank = psum.tile([P, UH], F32, name="colour", tag=tag, bufs=bufs)
-                nc.tensor.matmul_mx(out=bank[:], lhsT=w3_codes[:, m * P : (m + 1) * P].bitcast(FP8X4),
-                                    lhsT_scale=w3_scales[:, m * P : (m + 1) * P],
+            pair_total(ray_pairs[h], ray[LAST], 0.0, h * VH, (h + 1) * VH)
+        background(LAST)
+        for r0, r1 in PIECES:
+            fetch(ray_at, ray[LAST], LAST, r0, r1)
+
+        def blend(r0, r1):
+            hid = keep.tile([P, r1 - r0, PACK], BF16, name=f"hid{r0}", align_bytes=64)
+            nc.vector.tensor_tensor(hid[:].rearrange("p (c i) t -> p c t i", i=4),
+                                    shade[:, :, r0:r1].rearrange("p t (c i) -> p c t i", i=4),
+                                    ray_at[:, :, r0:r1].rearrange("p t (c i) -> p c t i", i=4), ALU.subtract)
+            return hid
+
+        def colours(hid, r0, r1):
+            codes, scales = quantise(f"hid{r0}", hid[:].rearrange("p r t -> p (r t)"))
+            for m, (tag, banks) in enumerate((("sd", SD_BANKS), ("ft", FT_BANKS))):
+                rows = slice(m * P, (m + 1) * P)
+                bank = psum.tile([P, r1 - r0], F32, name="colour", tag=tag, bufs=banks)
+                nc.tensor.matmul_mx(out=bank[:], lhsT=w3_codes[:, rows].bitcast(FP8X4), lhsT_scale=w3_scales[:, rows],
                                     rhs=codes[:].bitcast(FP8X4), rhs_scale=scales[:], start=True, stop=True)
-                result = keep.tile([P, UH], F32, name=f"result{h}{m}")
-                if h == 1 and m == 1:
+                result = keep.tile([P, r1 - r0], F32, name=f"result{r0}_{m}")
+                if r1 == U and m == 1:
                     nc.vector.tensor_copy(result[:], bank[:])
                 else:
                     nc.scalar.copy(result[:], bank[:])
-                nc.sync.dma_start(out[m * P : (m + 1) * P, h * UH : (h + 1) * UH], result[:])
+                nc.sync.dma_start(out[rows, r0:r1], result[:])
+
+        hids = [blend(*PIECES[0])]
+        for before, piece in zip(PIECES, PIECES[1:]):
+            hids.append(blend(*piece))
+            colours(hids[-2], *before)
+        colours(hids[-1], *PIECES[-1])

import math
from contextlib import ExitStack

import concourse.mybir as mybir
from concourse.masks import make_identity

K, T, S, D, N, H, V, U = 512, 4096, 1024, 4, 256, 512, 256, 512
FLOPS = 2 * (2 * K * H * S + H * N * U)

F32 = mybir.dt.float32
BF16 = mybir.dt.bfloat16
I32 = mybir.dt.int32
U32 = mybir.dt.uint32
U16 = mybir.dt.uint16
U8 = mybir.dt.uint8
FP8X4 = mybir.dt.float8_e4m3fn_x4
ACT = mybir.ActivationFunctionType
ALU = mybir.AluOpType

P = 128
PACK = 4
LAST = PACK - 1
PER_COLUMN = 16
HALF = S // 2
VH = V // 2
PAD = 8
WINDOW = U + 16
SD_BANKS, FT_BANKS, TURN_BANKS, BACK_BANKS = 3, 2, 2, 1
HEAD_ROWS, LAST_ROW = slice(0, D - 1), slice(D - 1, D)
PIECES = ((0, 128), (128, 384), (384, 512))


def tile_picked_yneusa_bg_p_kernel(tc, x_words, x_scales, w1, w2, bg, unit, w3, offs, pix, out):
    nc = tc.nc
    with ExitStack() as ctx:
        keep = ctx.enter_context(tc.tile_pool(name="keep", bufs=1))
        ring = ctx.enter_context(tc.tile_pool(name="ring", bufs=2))
        psum = ctx.enter_context(tc.psum_pool(name="psum", bufs=1))

        offs_sb = keep.tile([P, S // PER_COLUMN], U16, name="offs_sb")
        pix_sb = keep.tile([P, U // PER_COLUMN], U16, name="pix_sb")
        x_table = keep.tile([P, T], I32, name="x_table", align_bytes=64)
        s_table = keep.tile([P, T], U8, name="s_table", align_bytes=64)
        w1_raw = keep.tile([P, PACK, H], F32, name="w1_raw")
        w2_raw = keep.tile([P, PACK, H], F32, name="w2_raw")
        w3_raw = keep.tile([P, PACK, N], F32, name="w3_raw")
        bg_sb = keep.tile([P, PACK, U], F32, name="bg_sb")
        unit_sb = keep.tile([P, PACK], F32, name="unit_sb")

        nc.vector.memset(s_table[:].bitcast(I32), 0)
        nc.sync.dma_start(offs_sb[:], offs)
        nc.sync.dma_start(w1_raw[:], w1.rearrange("(p j) c -> p j c", j=PACK))
        for q in range(4):
            nc.sync.dma_start(s_table[32 * q : 32 * q + 4, :].bitcast(I32), x_scales[0, 4 * q : 4 * q + 4, :].bitcast(I32))
        nc.sync.dma_start(x_table[:], x_words[0].rearrange("p c r -> p (c r)").bitcast(I32))
        nc.sync.dma_start(w2_raw[:], w2.rearrange("(p j) c -> p j c", j=PACK))
        nc.sync.dma_start(unit_sb[:], unit.rearrange("(p t) o -> p (t o)", t=PACK))
        nc.sync.dma_start(pix_sb[:], pix)
        nc.sync.dma_start(bg_sb[:], bg.rearrange("(p t) r -> p t r", t=PACK))
        nc.sync.dma_start(w3_raw[:], w3.rearrange("(p j) c -> p j c", j=PACK))

        identity = keep.tile([P, P], F32, name="identity")
        make_identity(nc, identity[:])
        cdf = [keep.tile([P, D, V + PAD], F32, name=f"cdf{t}") for t in range(PACK)]
        alf_rows = [keep.tile([P, D + 1, PAD + V], F32, name=f"alf{t}") for t in range(PACK)]
        alf = [rows[:, 1:, :] for rows in alf_rows]
        ray = [keep.tile([P, WINDOW], F32, name=f"ray{t}") for t in range(PACK)]
        rest = [keep.tile([P, WINDOW], F32, name=f"rest{t}") for t in range(PACK)]
        for t in range(PACK):
            nc.gpsimd.memset(cdf[t][:, 0, V : V + 1], 0.0)
            nc.gpsimd.memset(alf[t][:, D - 1, PAD - 1 : PAD], 10.0)
            nc.gpsimd.memset(ray[t][:, (2 * V if t + 1 < LAST else V) :], 0.0)
            nc.gpsimd.memset(rest[t][:, (2 * V if t < LAST else V) :], 0.0)
        first_staged = keep.tile([P, V], F32, name="first_staged")

        def quantise(name, grouped):
            columns = grouped.shape[1] // PACK
            codes = keep.tile([P, columns], U32, name=name + "_codes", align_bytes=64)
            scales = keep.tile([P, columns], U8, name=name + "_scales", align_bytes=64)
            nc.vector.quantize_mx(out=codes[:].bitcast(FP8X4), scales=scales[:], in_=grouped)
            return codes, scales

        def deal_plane_pair(name, raw, t0, round_copy):
            grouped = keep.tile([P, 2, P, PACK], BF16, name=name + "_bf", align_bytes=64)
            round_copy(
                grouped[:].rearrange("p t m j -> p m j t"),
                raw[:].rearrange("p j (m t) -> p m j t", t=PACK)[:, :, :, t0 : t0 + 2],
            )
            codes, scales = quantise(name, grouped[:].rearrange("p t m j -> p (t m j)"))
            return [(codes[:, i * P : (i + 1) * P], scales[:, i * P : (i + 1) * P]) for i in range(2)]

        w1_q = deal_plane_pair("w1a", w1_raw, 0, nc.vector.tensor_copy) + deal_plane_pair("w1b", w1_raw, 2, nc.vector.tensor_copy)

        picked = {}
        for h in (1, 0):
            words = keep.tile([P, HALF], U32, name=f"words{h}", align_bytes=64)
            scale_bytes = keep.tile([P, HALF], U8, name=f"bytes{h}", align_bytes=64)
            entries = offs_sb[:, h * HALF // PER_COLUMN : (h + 1) * HALF // PER_COLUMN]
            nc.vector.tensor_copy(words[:], x_table[:].bitcast(U32).indirect(entries))
            nc.vector.tensor_copy(scale_bytes[:], s_table[:].indirect(entries))
            picked[h] = (words, scale_bytes)

        def product(weight, h, tag, banks):
            bank = psum.tile([P, HALF], F32, name=tag, tag=tag, bufs=banks)
            words, scale_bytes = picked[h]
            nc.tensor.matmul_mx(out=bank[:], lhsT=weight[0].bitcast(FP8X4), lhsT_scale=weight[1],
                                rhs=words[:].bitcast(FP8X4), rhs_scale=scale_bytes[:], start=True, stop=True)
            return bank[:].rearrange("p (v d) -> p d v", d=D)

        tail, fall, nwe, wf = {}, {}, {}, {}

        def sigmoids(t):
            tail[t] = ring.tile([P, D, V], F32, name="tail")
            for h in (1, 0):
                sd = product(w1_q[t], h, "sd", SD_BANKS)
                rays = slice(h * VH, (h + 1) * VH)
                nc.scalar.activation(tail[t][:, :, rays], sd, ACT.Sigmoid, scale=-2.5, bias=-math.log(11.0))
                nc.scalar.activation(cdf[t][:, :, rays], sd, ACT.Sigmoid, scale=2.5)

        def inverse(engine, inv, tail_part):
            engine.tensor_scalar(inv, tail_part, -1000.0 / 11.0, -100.0 / 11.0, ALU.mult, ALU.add)

        def ratio(t, inv_head, inv_last, v0, v1):
            if t not in fall:
                fall[t] = ring.tile([P, D, V], F32, name="fall")
            nc.vector.scalar_tensor_tensor(fall[t][:, HEAD_ROWS, v0:v1], cdf[t][:, 1:, v0:v1], 0.1, inv_head[:, :, v0:v1], ALU.add, ALU.mult)
            nc.vector.scalar_tensor_tensor(fall[t][:, D - 1, v0:v1], cdf[t][:, 0, v0 + 1 : v1 + 1], 0.1, inv_last[:, v0:v1], ALU.add, ALU.mult)

        def opacity(t, v0, v1, row_runs):
            for rows in row_runs:
                nc.vector.scalar_tensor_tensor(alf[t][:, rows, PAD + v0 : PAD + v1], fall[t][:, rows, v0:v1], 10.0, cdf[t][:, rows, v0:v1], ALU.add, ALU.max)

        def weights(t):
            nwe[t] = ring.tile([P, D, V], F32, name="nwe")
            nc.vector.scalar_tensor_tensor(nwe[t][:, 1:3, :], alf[t][:, 0:2, PAD:], 10.0, alf[t][:, 1:3, PAD:], ALU.subtract, ALU.mult)
            nc.vector.scalar_tensor_tensor(nwe[t][:, 0, :], alf[t][:, D - 1, PAD - 1 : PAD - 1 + V], 10.0, alf[t][:, 0, PAD:], ALU.subtract, ALU.mult)
            nc.vector.scalar_tensor_tensor(nwe[t][:, 3, :], alf[t][:, 2, PAD:], 10.0, alf[t][:, 3, PAD:], ALU.subtract, ALU.mult)

        def weighted_features(t):
            wf[t] = ring.tile([P, D, V], F32, name="wf")
            ft = [product(w2_q[t], h, "ft", FT_BANKS) for h in range(2)]
            for rows in (HEAD_ROWS, LAST_ROW):
                for h in range(2):
                    rays = slice(h * VH, (h + 1) * VH)
                    nc.vector.tensor_tensor(wf[t][:, rows, rays], nwe[t][:, rows, rays], ft[h][:, rows, :], ALU.mult)

        def turned_sum(members, window, scale, offset, staged):
            turned = psum.tile([P, 2, P], F32, name="turned", tag="turned", bufs=TURN_BANKS)
            for h in range(2):
                for d in range(D):
                    nc.tensor.matmul(turned[:, h, :], members[:, d, h * VH : (h + 1) * VH], identity[:],
                                     start=(d == 0), stop=(d == D - 1), is_transpose=True)
            nc.scalar.copy(staged, turned[:].rearrange("p h i -> p (h i)"))
            back = psum.tile([P, 2, P], F32, name="back", tag="back", bufs=BACK_BANKS)
            for h in range(2):
                nc.tensor.transpose(back[:, h, :], staged[:, h * P : (h + 1) * P], identity[:])
            nc.scalar.activation(window[:, :V], back[:].rearrange("p h v -> p (h v)"), ACT.Copy, scale=scale, bias=offset)

        ray_at = keep.tile([P, PACK, U], F32, name="ray_at")
        rest_at = keep.tile([P, PACK, U], F32, name="rest_at")
        shade = keep.tile([P, PACK, U], F32, name="shade")

        def fetch(target, window, t, r0, r1):
            nc.scalar.activation(target[:, t, r0:r1], window[:].indirect(pix_sb[:, r0 // PER_COLUMN : r1 // PER_COLUMN]), ACT.Copy)

        def background(t):
            nc.vector.scalar_tensor_tensor(shade[:, t, :], rest_at[:, t, :], unit_scale[:, t : t + 1], bg_sb[:, t, :], ALU.mult, ALU.mult)

        def pair_sum(members, v0, v1):
            pairs = ring.tile([P, 2, v1 - v0], F32, name="pairs", bufs=3)
            nc.vector.tensor_tensor(pairs[:], members[:, :2, v0:v1], members[:, 2:, v0:v1], ALU.add)
            return pairs

        def pair_total(pairs, window, offset, v0, v1):
            nc.vector.scalar_tensor_tensor(window[:, v0:v1], pairs[:, 0, :], offset, pairs[:, 1, :], ALU.add, ALU.add)

        sigmoids(0)
        w2_q = deal_plane_pair("w2a", w2_raw, 0, nc.scalar.copy)
        unit_scale = keep.tile([P, PACK], F32, name="unit_scale")
        nc.gpsimd.tensor_scalar(unit_scale[:], unit_sb[:], 0.01, 0.0, ALU.mult, ALU.add)
        inv_first = keep.tile([P, D, V], F32, name="inv_first")
        inverse(nc.vector, inv_first[:, :, VH:], tail[0][:, :, VH:])
        ratio(0, inv_first[:, HEAD_ROWS, :], inv_first[:, D - 1, :], VH, V)
        inverse(nc.vector, inv_first[:, :, :VH], tail[0][:, :, :VH])
        opacity(0, VH, V, (slice(0, D),))
        ratio(0, inv_first[:, HEAD_ROWS, :], inv_first[:, D - 1, :], 0, VH)
        opacity(0, 0, VH, (HEAD_ROWS, LAST_ROW))
        sigmoids(1)

        for t in range(LAST):
            weights(t)
            inv_head = alf_rows[t][:, HEAD_ROWS, PAD:]
            inverse(nc.gpsimd, inv_head, tail[t + 1][:, HEAD_ROWS, :])
            weighted_features(t)
            inv_last = ring.tile([P, V], F32, name="inv_last")
            inverse(nc.vector, inv_last[:], tail[t + 1][:, D - 1, :])
            turned_sum(nwe[t], rest[t], 1.0, 100.0, ray[t - 1][:, V : 2 * V] if t >= 1 else first_staged[:])
            if t >= 1:
                fetch(ray_at, ray[t - 1], t - 1, 0, U)
            if t + 2 <= LAST:
                sigmoids(t + 2)
            ratio(t + 1, inv_head, inv_last, 0, V)
            if t >= 1:
                background(t - 1)
            opacity(t + 1, 0, V, (HEAD_ROWS, LAST_ROW))
            turned_sum(wf[t], ray[t], unit_scale[:, t : t + 1], 0.0, rest[t][:, V : 2 * V])
            fetch(rest_at, rest[t], t, 0, U)
            if t == 0:
                w2_q = w2_q + deal_plane_pair("w2b", w2_raw, 2, nc.scalar.copy)

        w3_bf = keep.tile([P, N, PACK], BF16, name="w3_bf", align_bytes=64)
        nc.scalar.copy(w3_bf[:].rearrange("p (c i) j -> p c j i", i=4), w3_raw[:].rearrange("p j (c i) -> p c j i", i=4))
        w3_codes, w3_scales = quantise("w3", w3_bf[:].rearrange("p n j -> p (n j)"))

        fetch(ray_at, ray[LAST - 1], LAST - 1, 0, U)
        weights(LAST)
        background(LAST - 1)
        wf[LAST] = ring.tile([P, D, V], F32, name="wf")

        def weighted_features_last(h):
            ft = product(w2_q[LAST], h, "ft", FT_BANKS)
            rays = slice(h * VH, (h + 1) * VH)
            nc.vector.scalar_tensor_tensor(wf[LAST][:, :, rays], nwe[LAST][:, :, rays], unit_scale[:, LAST : LAST + 1], ft, ALU.mult, ALU.mult)

        rest_pairs = pair_sum(nwe[LAST], 0, V)
        weighted_features_last(0)
        pair_total(rest_pairs, rest[LAST], 100.0, 0, V)
        fetch(rest_at, rest[LAST], LAST, 0, U)
        weighted_features_last(1)
        ray_pairs = [pair_sum(wf[LAST], h * VH, (h + 1) * VH) for h in range(2)]
        for h in range(2):
            pair_total(ray_pairs[h], ray[LAST], 0.0, h * VH, (h + 1) * VH)
        background(LAST)
        for r0, r1 in PIECES:
            fetch(ray_at, ray[LAST], LAST, r0, r1)

        def blend(r0, r1):
            hid = keep.tile([P, r1 - r0, PACK], BF16, name=f"hid{r0}", align_bytes=64)
            nc.vector.tensor_tensor(hid[:].rearrange("p (c i) t -> p c t i", i=4),
                                    shade[:, :, r0:r1].rearrange("p t (c i) -> p c t i", i=4),
                                    ray_at[:, :, r0:r1].rearrange("p t (c i) -> p c t i", i=4), ALU.subtract)
            return hid

        def colours(hid, r0, r1):
            codes, scales = quantise(f"hid{r0}", hid[:].rearrange("p r t -> p (r t)"))
            for m, (tag, banks) in enumerate((("sd", SD_BANKS), ("ft", FT_BANKS))):
                rows = slice(m * P, (m + 1) * P)
                bank = psum.tile([P, r1 - r0], F32, name="colour", tag=tag, bufs=banks)
                nc.tensor.matmul_mx(out=bank[:], lhsT=w3_codes[:, rows].bitcast(FP8X4), lhsT_scale=w3_scales[:, rows],
                                    rhs=codes[:].bitcast(FP8X4), rhs_scale=scales[:], start=True, stop=True)
                result = keep.tile([P, r1 - r0], F32, name=f"result{r0}_{m}")
                if r1 == U and m == 1:
                    nc.vector.tensor_copy(result[:], bank[:])
                else:
                    nc.scalar.copy(result[:], bank[:])
                nc.sync.dma_start(out[rows, r0:r1], result[:])

        hids = [blend(*PIECES[0])]
        for before, piece in zip(PIECES, PIECES[1:]):
            hids.append(blend(*piece))
            colours(hids[-2], *before)
        colours(hids[-1], *PIECES[-1])
